import numpy as np
import ml_dtypes


def mxq(x, axis, fmt="e4m3"):
    dtype, down = {"e4m3": (ml_dtypes.float8_e4m3fn, 7), "e5m2": (ml_dtypes.float8_e5m2, 14)}[fmt]
    v = np.moveaxis(np.asarray(x, np.float32).astype(ml_dtypes.bfloat16).astype(np.float64), axis, -1)
    blocks = v.reshape(v.shape[:-1] + (-1, 32))
    amax = np.abs(blocks).max(-1, keepdims=True)
    byte = np.maximum(np.where(amax > 0, np.frexp(amax)[1] - 1 + 127, 0) - down, 1)
    scale = np.exp2(byte - 127.0)
    codes = (blocks / scale).astype(np.float32).astype(dtype).astype(np.float64)
    return np.moveaxis((codes * scale).reshape(v.shape), -1, axis)


WIDE = False


def mx_kscale(k):
    if not WIDE:
        return np.ones(k)
    levels = np.array([10, -10, 5, -5, 0])
    if k % 512:
        return np.exp2(np.random.permutation(np.resize(levels, k // 32))).repeat(32)
    a = np.empty((k // 512, 16))
    for p in range(k // 512):
        a[p, :8] = np.random.permutation(np.resize(levels, 8))
        for g in range(8):
            far = levels[np.abs(levels - a[p, g]) >= 10]
            a[p, g + 8] = far[np.random.randint(len(far))]
    return np.exp2(a.ravel()).repeat(32)


def f64(x):
    return np.asarray(x).astype(np.float64)


def striped(idx):
    return np.tile(np.asarray(idx).reshape(-1, 16).T, (8, 1)).astype(np.uint16)


def unstriped(offs):
    return offs[:16].T.reshape(-1).astype(np.int64)


E2M1 = np.array([0.0, 0.5, 1.0, 1.5, 2.0, 3.0, 4.0, 6.0, -0.0, -0.5, -1.0, -1.5, -2.0, -3.0, -4.0, -6.0])


def pack_weight(w, fmt):
    k, n = w.shape
    w = f64(np.asarray(w, np.float32).astype(ml_dtypes.bfloat16)).reshape(k // 32, 32, n)
    amax = np.abs(w).max(1)
    if fmt == "e4m3":
        byte = np.frexp(amax)[1] - 1 + 127 - 7
    else:
        mant, ex = np.frexp(amax / 6.0)
        byte = np.where(mant > 0.5, ex, ex - 1) + 127
    byte = np.clip(np.where(amax > 0, byte, 1), 1, 254)
    scaled = (w * np.exp2(127.0 - byte)[:, None, :]).reshape(k, n).astype(np.float32)
    by_word = np.ascontiguousarray(scaled.reshape(k // 512, 128, 4, n).transpose(0, 1, 3, 2))
    if fmt == "e4m3":
        words = by_word.astype(ml_dtypes.float8_e4m3fn).view(np.uint8)
    else:
        c = by_word.astype(ml_dtypes.float4_e2m1fn).view(np.uint8) & 0xF
        words = (c[..., 0::2] | (c[..., 1::2] << 4)).reshape(k // 512, 128, 2 * n)
    return np.ascontiguousarray(words), np.ascontiguousarray(byte.astype(np.uint8).reshape(k // 512, 16, n))


def unpack_weight(words, scales, fmt):
    g, _, n = scales.shape
    words = np.ascontiguousarray(words).reshape(g, 128, n, -1)
    if fmt == "e4m3":
        vals = words.view(ml_dtypes.float8_e4m3fn).astype(np.float64)
    else:
        nib = np.empty((g, 128, n, 4), np.uint8)
        nib[..., 0::2] = words & 0xF
        nib[..., 1::2] = words >> 4
        vals = E2M1[nib]
    vals = vals * np.repeat(np.exp2(scales.astype(np.float64) - 127.0), 8, axis=1)[..., None]
    return vals.transpose(0, 1, 3, 2).reshape(g * 512, n)


def bf(x):
    return np.asarray(x, np.float32).astype(ml_dtypes.bfloat16)


def planes(Y):
    r, m = Y.shape
    b = f64(bf(Y)).reshape(r // 32, 32, m)
    amax = np.abs(b).max(1)
    byte = np.clip(np.where(amax > 0, np.frexp(amax)[1] - 1 + 127 - 7, 1), 1, 254)
    codes = (b * np.exp2(127.0 - byte)[:, None, :]).reshape(r, m).astype(np.float32).astype(ml_dtypes.float8_e4m3fn).view(np.uint8)
    words = codes.reshape(r // 512, 128, 4, m).transpose(0, 1, 3, 2)
    return np.ascontiguousarray(words), np.ascontiguousarray(byte.astype(np.uint8).reshape(r // 512, 16, m))


D, T, I, Q, E, K = 512, 2048, 512, 256, 512, 512


def setup_inputs():
    n = np.random.standard_normal
    idx = np.random.permutation(T)[:I]
    fd = mx_kscale(D)
    fk = mx_kscale(K)
    fi = mx_kscale(I)
    ti = np.ones(T)
    ti[idx] = fi
    keysp = pack_weight(n((D, T)) / fd[:, None], "e2m1")
    return {
        "query": (n((D, Q)) * 0.4 / np.sqrt(D) * fd[:, None]).astype(np.float32),
        "query2": (n((K, Q)) * 0.4 / np.sqrt(K) * fk[:, None]).astype(np.float32),
        "keys_words": keysp[0],
        "keys_scales": keysp[1],
        "keys2": (n((K, T)) / fk[:, None]).astype(np.float32),
        "size": (np.random.uniform(0.5, 2.0, (1, I)) * fi).astype(np.float32),
        "vals": (n((E, T)) / ti).astype(np.float32),
        "offs": striped(idx),
    }


def reference(query, query2, keys_words, keys_scales, keys2, size, vals, offs):
    idx = unstriped(offs)
    keysu = unpack_weight(keys_words, keys_scales, "e2m1")
    queryq = mxq(f64(query), 0, "e4m3")
    keysidxg = keysu[:, idx]
    a = queryq.T @ keysidxg
    query2q = mxq(f64(query2), 0, "e4m3")
    keys2idxq = mxq(f64(keys2)[:, idx], 0, "e4m3")
    b = query2q.T @ keys2idxq
    s = np.maximum(a, b) + np.minimum(a, b) * 0.5
    p = np.exp(s - np.max(s, axis=1, keepdims=True))
    w = p * f64(size) / np.sum(p, axis=1, keepdims=True)
    wt = w.T
    vt = f64(vals)[:, idx].T
    vtq = mxq(vt, 0, "e4m3")
    wtq = mxq(wt, 0, "e4m3")
    o = vtq.T @ wtq
    words, scales = planes(o)
    return o, words, scales

@@ -1,0 +1,222 @@
+from contextlib import ExitStack
+
+import concourse.mybir as mybir
+from concourse.masks import make_identity
+
+D, T, I, Q, E, K = 512, 2048, 512, 256, 512, 512
+FLOPS = 2 * Q * I * (D + K + E)
+
+F32 = mybir.dt.float32
+BF16 = mybir.dt.bfloat16
+I32 = mybir.dt.int32
+U32 = mybir.dt.uint32
+U16 = mybir.dt.uint16
+U8 = mybir.dt.uint8
+FP8X4 = mybir.dt.float8_e4m3fn_x4
+FP4X4 = mybir.dt.float4_e2m1fn_x4
+ALU = mybir.AluOpType
+ACT = mybir.ActivationFunctionType
+AXIS_X = mybir.AxisListType.X
+
+P = 128
+PACK = 4
+QT = Q // P
+ST = I // P
+HALF = I // 2
+
+
+def tile_attend_bestofviews_pl_kernel(
+    tc, query, query2, keys_words, keys_scales, keys2, size, vals, offs, out_0, out_1, out_2
+):
+    nc = tc.nc
+    with ExitStack() as ctx:
+        sb = ctx.enter_context(tc.tile_pool(name="sb", bufs=1))
+        ps = ctx.enter_context(tc.psum_pool(name="ps", bufs=1))
+
+        def tile(name, shape, dtype):
+            return sb.tile(shape, dtype, name=name, align_bytes=64)
+
+        def bank(n, name, shape):
+            return ps.tile(shape, F32, name=name, tag="bank%d" % n)
+
+        def quantize(name, grouped, width):
+            codes = tile(name + "_codes", [P, width], U32)
+            scales = tile(name + "_scales", [P, width], U8)
+            nc.vector.quantize_mx(
+                out=codes[:].bitcast(FP8X4), scales=scales[:], in_=grouped[:].rearrange("p c t -> p (c t)")
+            )
+            return codes, scales
+
+        def interleave(dst, src):
+            nc.scalar.copy(
+                dst.rearrange("p (c i) t -> p c t i", i=4), src.rearrange("p t (c i) -> p c t i", i=4)
+            )
+
+        offsets = sb.tile([P, I // 16], U16, name="offsets")
+        kw_pool = tile("kw_pool", [P, T], U16)
+        ks_pool = tile("ks_pool", [P, T], U8)
+        size_col = tile("size_col", [P, PACK], F32)
+        q_raw = tile("q_raw", [P, PACK, Q], F32)
+        q2_raw = tile("q2_raw", [P, PACK, Q], F32)
+        k2_pool = [tile("k2_pool%d" % t, [P, T], F32) for t in range(PACK)]
+        v_pool = [tile("v_pool%d" % t, [P, T], F32) for t in range(PACK)]
+        k2_rows = keys2.rearrange("(p t) c -> t p c", t=PACK)
+        v_rows = vals.rearrange("(p t) c -> t p c", t=PACK)
+
+        nc.sync.dma_start(kw_pool[:].bitcast(I32), keys_words[0].bitcast(I32))
+        nc.sync.dma_start(offsets[:], offs)
+        nc.sync.dma_start(q_raw[:], query.rearrange("(p t) q -> p t q", t=PACK))
+        nc.sync.dma_start(size_col[:], size[0].rearrange("(p t) -> p t", t=PACK))
+        for t in range(PACK):
+            nc.sync.dma_start(k2_pool[t][:], k2_rows[t])
+        nc.sync.dma_start(q2_raw[:], query2.rearrange("(p t) q -> p t q", t=PACK))
+        for t in range(PACK):
+            nc.sync.dma_start(v_pool[t][:], v_rows[t])
+
+        nc.vector.memset(ks_pool[:].bitcast(I32), 0)
+        for quad in range(4):
+            nc.scalar.dma_start(
+                ks_pool[32 * quad : 32 * quad + 4, :].bitcast(I32),
+                keys_scales[0, 4 * quad : 4 * quad + 4, :].bitcast(I32),
+            )
+        ident = tile("ident", [P, P], F32)
+        make_identity(nc, ident[:])
+
+        kw = tile("kw", [P, I], U16)
+        nc.vector.tensor_copy(kw[:], kw_pool[:].indirect(offsets[:]))
+        q_grp = tile("q_grp", [P, Q, PACK], BF16)
+        interleave(q_grp[:], q_raw[:])
+        q_codes, q_scales = quantize("q", q_grp, Q)
+        ks = tile("ks", [P, I], U8)
+        nc.vector.tensor_copy(ks[:], ks_pool[:].indirect(offsets[:]))
+
+        size_ps = bank(6, "size_ps", [P, PACK, P])
+        for t in range(PACK):
+            nc.tensor.transpose(size_ps[:, t, :], size_col[:, t : t + 1].to_broadcast([P, P]), ident[:])
+        size_row = tile("size_row", [P, P, PACK], F32)
+        nc.scalar.copy(size_row[:], size_ps[:].rearrange("m t p -> m p t"))
+
+        s_ps = [bank(4 + x, "s_ps%d" % x, [P, I]) for x in range(QT)]
+        half_a = [tile("half_a%d" % j, [P, Q], F32) for j in range(ST)]
+        for j in range(ST):
+            cols = slice(j * P, (j + 1) * P)
+            a_ps = bank(j, "a_ps%d" % j, [P, Q])
+            nc.tensor.matmul_mx(
+                out=a_ps[:], lhsT=kw[:, cols].bitcast(FP4X4), lhsT_scale=ks[:, cols],
+                rhs=q_codes[:].bitcast(FP8X4), rhs_scale=q_scales[:], start=True, stop=True,
+            )
+            nc.scalar.activation(half_a[j][:], a_ps[:], ACT.Copy, scale=0.5)
+
+        def add_turned(x, j, src, start, stop):
+            nc.tensor.matmul(
+                s_ps[x][:, j * P : (j + 1) * P], src[:, x * P : (x + 1) * P], ident[:],
+                start=start, stop=stop, is_transpose=True,
+            )
+
+        for x in range(QT):
+            for j in range(ST):
+                add_turned(x, j, half_a[j], j == 0, False)
+
+        k2_grp = [tile("k2_grp%d" % h, [P, HALF, PACK], BF16) for h in range(2)]
+        for t in range(PACK):
+            for h in range(2):
+                nc.vector.tensor_copy(
+                    k2_grp[h][:, :, t], k2_pool[t][:].indirect(offsets[:, h * 16 : (h + 1) * 16])
+                )
+        k2_q = [quantize("k2_%d" % h, k2_grp[h], HALF) for h in range(2)]
+        q2_grp = tile("q2_grp", [P, Q, PACK], BF16)
+        interleave(q2_grp[:], q2_raw[:])
+        q2_codes, q2_scales = quantize("q2", q2_grp, Q)
+
+        half_b = [tile("half_b%d" % j, [P, Q], F32) for j in range(ST)]
+        half_m = [tile("half_m%d" % j, [P, Q], F32) for j in range(ST)]
+        for j in range(ST):
+            codes, scales = k2_q[j // 2]
+            cols = slice((j % 2) * P, (j % 2 + 1) * P)
+            b_ps = bank(j, "b_ps%d" % j, [P, Q])
+            nc.tensor.matmul_mx(
+                out=b_ps[:], lhsT=codes[:, cols].bitcast(FP8X4), lhsT_scale=scales[:, cols],
+                rhs=q2_codes[:].bitcast(FP8X4), rhs_scale=q2_scales[:], start=True, stop=True,
+            )
+            nc.vector.scalar_tensor_tensor(half_m[j][:], b_ps[:], 0.5, half_a[j][:], ALU.mult, ALU.max)
+            nc.scalar.activation(half_b[j][:], b_ps[:], ACT.Copy, scale=0.5)
+        for x in range(QT):
+            for j in range(ST):
+                add_turned(x, j, half_m[j], False, False)
+                add_turned(x, j, half_b[j], False, j == ST - 1)
+
+        def turn_pairs(name, n, src):
+            words = src[:].bitcast(F32)
+            turned = bank(n, name + "_ps", [P, 2, P])
+            for u in range(2):
+                nc.tensor.transpose(turned[:, u, :], words[:, u : I // 2 : 2], ident[:])
+            grouped = tile(name + "_grp", [P, P, PACK], BF16)
+            nc.scalar.copy(grouped[:].bitcast(F32), turned[:].rearrange("p u c -> p c u"))
+            return grouped
+
+        def gather_values(t):
+            picked = tile("v_picked%d" % t, [P, I], BF16)
+            nc.vector.tensor_copy(picked[:], v_pool[t][:].indirect(offsets[:]))
+            return turn_pairs("v%d" % t, 6 + t % 2, picked)
+
+        def exponentials(x):
+            neg_max = tile("neg_max%d" % x, [P, 1], F32)
+            nc.vector.tensor_reduce(neg_max[:], s_ps[x][:], AXIS_X, ALU.max, negate=True)
+            p = tile("p%d" % x, [P, I], F32)
+            total = tile("total%d" % x, [P, 1], F32)
+            nc.scalar.activation(p[:], s_ps[x][:], ACT.Exp, bias=neg_max[:], accum_out=total[:])
+            return p, total
+
+        def weights(x, p, total):
+            inv = tile("inv%d" % x, [P, 1], F32)
+            nc.vector.reciprocal(inv[:], total[:])
+            w = tile("w%d" % x, [P, I], BF16)
+            nc.vector.scalar_tensor_tensor(
+                w[:], p[:], inv[:], size_row[:].rearrange("m p t -> m (p t)"), ALU.mult, ALU.mult
+            )
+            return turn_pairs("w%d" % x, 2 + x, w)
+
+        v_grp = [gather_values(0)]
+        exps = [exponentials(x) for x in range(QT)]
+        v_grp.append(gather_values(1))
+        w_grp = [weights(x, *exps[x]) for x in range(QT)]
+        v_q = [quantize("v%d" % t, v_grp[t], P) for t in range(2)]
+        v_grp.append(gather_values(2))
+        w_q = [quantize("w%d" % x, w_grp[x], P) for x in range(QT)]
+        v_grp.append(gather_values(3))
+        v_q.append(quantize("v2", v_grp[2], P))
+
+        o_ps = [bank(x, "o_ps%d" % x, [P, PACK, P]) for x in range(QT)]
+        o_early = tile("o_early", [P, PACK - 1, Q], F32)
+        o_last = tile("o_last", [P, Q], F32)
+        out_rows = out_0.rearrange("(p t) q -> p t q", t=PACK)
+
+        def product(x, t):
+            nc.tensor.matmul_mx(
+                out=o_ps[x][:, t, :], lhsT=v_q[t][0][:].bitcast(FP8X4), lhsT_scale=v_q[t][1][:],
+                rhs=w_q[x][0][:].bitcast(FP8X4), rhs_scale=w_q[x][1][:], start=True, stop=True,
+            )
+
+        for x in range(QT):
+            for t in range(PACK - 1):
+                product(x, t)
+            nc.scalar.copy(o_early[:, :, x * P : (x + 1) * P], o_ps[x][:, 0 : PACK - 1, :])
+        nc.sync.dma_start(out_rows[:, 0 : PACK - 1, :], o_early[:])
+
+        v_q.append(quantize("v3", v_grp[3], P))
+        for x in range(QT):
+            product(x, PACK - 1)
+        o_grp = tile("o_grp", [P, Q, PACK], BF16)
+        nc.vector.tensor_copy(o_grp[:, 0:P, :], o_ps[0][:].rearrange("p t q -> p q t"))
+        nc.scalar.copy(o_grp[:, P:Q, :], o_ps[1][:].rearrange("p t q -> p q t"))
+        o_codes, o_scales = quantize("o", o_grp, Q)
+        for x in (1, 0):
+            nc.scalar.copy(o_last[:, x * P : (x + 1) * P], o_ps[x][:, PACK - 1, :])
+        nc.scalar.dma_start(out_rows[:, PACK - 1, :], o_last[:])
+        nc.sync.dma_start(out_1[0].rearrange("p c r -> p (c r)").bitcast(I32), o_codes[:].bitcast(I32))
+        for quad in range(4):
+            queue = nc.sync if quad < 2 else nc.scalar
+            queue.dma_start(
+                out_2[0, 4 * quad : 4 * quad + 4, :].bitcast(I32),
+                o_scales[32 * quad : 32 * quad + 4, :].bitcast(I32),
+            )

@@ -33,14 +33,14 @@ def tile_attend_bestofviews_pl_kernel(
         sb = ctx.enter_context(tc.tile_pool(name="sb", bufs=1))
         ps = ctx.enter_context(tc.psum_pool(name="ps", bufs=1))
 
-        def tile(name, shape, dtype):
-            return sb.tile(shape, dtype, name=name, align_bytes=64)
+        def tile(name, shape, dtype, after=None):
+            return sb.tile(shape, dtype, name=name, tag=after or name, align_bytes=64)
 
         def bank(n, name, shape):
             return ps.tile(shape, F32, name=name, tag="bank%d" % n)
 
-        def quantize(name, grouped, width):
-            codes = tile(name + "_codes", [P, width], U32)
+        def quantize(name, grouped, width, after=None):
+            codes = tile(name + "_codes", [P, width], U32, after)
             scales = tile(name + "_scales", [P, width], U8)
             nc.vector.quantize_mx(
                 out=codes[:].bitcast(FP8X4), scales=scales[:], in_=grouped[:].rearrange("p c t -> p (c t)")
@@ -93,8 +93,8 @@ def tile_attend_bestofviews_pl_kernel(
         size_ps = bank(6, "size_ps", [P, PACK, P])
         for t in range(PACK):
             nc.tensor.transpose(size_ps[:, t, :], size_col[:, t : t + 1].to_broadcast([P, P]), ident[:])
-        size_row = tile("size_row", [P, P, PACK], F32)
-        nc.scalar.copy(size_row[:], size_ps[:].rearrange("m t p -> m p t"))
+        size_row = tile("size_row", [P, 2, P, 2], F32)
+        nc.scalar.copy(size_row[:], size_ps[:].rearrange("m (u e) p -> m u p e", u=2))
 
         s_ps = [bank(4 + x, "s_ps%d" % x, [P, I]) for x in range(QT)]
         half_a = [tile("half_a%d" % j, [P, Q], F32) for j in range(ST)]
@@ -124,9 +124,16 @@ def tile_attend_bestofviews_pl_kernel(
                     k2_grp[h][:, :, t], k2_pool[t][:].indirect(offsets[:, h * 16 : (h + 1) * 16])
                 )
         k2_q = [quantize("k2_%d" % h, k2_grp[h], HALF) for h in range(2)]
-        q2_grp = tile("q2_grp", [P, Q, PACK], BF16)
-        interleave(q2_grp[:], q2_raw[:])
-        q2_codes, q2_scales = quantize("q2", q2_grp, Q)
+        q2_codes = tile("q2_codes", [P, Q], U32)
+        q2_scales = tile("q2_scales", [P, Q], U8)
+        for x in range(QT):
+            cols = slice(x * P, (x + 1) * P)
+            q2_grp = tile("q2_grp%d" % x, [P, P, PACK], BF16)
+            interleave(q2_grp[:], q2_raw[:, :, cols])
+            nc.vector.quantize_mx(
+                out=q2_codes[:, cols].bitcast(FP8X4), scales=q2_scales[:, cols],
+                in_=q2_grp[:].rearrange("p c t -> p (c t)"),
+            )
 
         half_b = [tile("half_b%d" % j, [P, Q], F32) for j in range(ST)]
         half_m = [tile("half_m%d" % j, [P, Q], F32) for j in range(ST)]
@@ -145,74 +152,108 @@ def tile_attend_bestofviews_pl_kernel(
                 add_turned(x, j, half_m[j], False, False)
                 add_turned(x, j, half_b[j], False, j == ST - 1)
 
-        def turn_pairs(name, n, src):
-            words = src[:].bitcast(F32)
+        def turn_pairs(name, n, halves, grouped):
             turned = bank(n, name + "_ps", [P, 2, P])
             for u in range(2):
-                nc.tensor.transpose(turned[:, u, :], words[:, u : I // 2 : 2], ident[:])
-            grouped = tile(name + "_grp", [P, P, PACK], BF16)
-            nc.scalar.copy(grouped[:].bitcast(F32), turned[:].rearrange("p u c -> p c u"))
-            return grouped
+                nc.tensor.transpose(turned[:, u, :], halves[u], ident[:])
+            nc.scalar.copy(grouped.bitcast(F32), turned[:].rearrange("p u c -> p c u"))
 
-        def gather_values(t):
+        def gather_values(t, after=None):
             picked = tile("v_picked%d" % t, [P, I], BF16)
             nc.vector.tensor_copy(picked[:], v_pool[t][:].indirect(offsets[:]))
-            return turn_pairs("v%d" % t, 6 + t % 2, picked)
+            return picked
 
-        def exponentials(x):
-            neg_max = tile("neg_max%d" % x, [P, 1], F32)
-            nc.vector.tensor_reduce(neg_max[:], s_ps[x][:], AXIS_X, ALU.max, negate=True)
+        def exponentials(x, neg_max, total):
+            nc.vector.tensor_reduce(neg_max, s_ps[x][:], AXIS_X, ALU.max, negate=True)
             p = tile("p%d" % x, [P, I], F32)
-            total = tile("total%d" % x, [P, 1], F32)
-            nc.scalar.activation(p[:], s_ps[x][:], ACT.Exp, bias=neg_max[:], accum_out=total[:])
-            return p, total
+            nc.scalar.activation(
+                p[:].rearrange("m (u p e) -> m u p e", u=2, e=2),
+                s_ps[x][:].rearrange("m (p u e) -> m u p e", u=2, e=2),
+                ACT.Exp, bias=neg_max, accum_out=total,
+            )
+            return p
 
-        def weights(x, p, total):
-            inv = tile("inv%d" % x, [P, 1], F32)
-            nc.vector.reciprocal(inv[:], total[:])
+        def weights(x, p, inv):
             w = tile("w%d" % x, [P, I], BF16)
             nc.vector.scalar_tensor_tensor(
-                w[:], p[:], inv[:], size_row[:].rearrange("m p t -> m (p t)"), ALU.mult, ALU.mult
+                w[:], p[:], inv, size_row[:].rearrange("m u p e -> m (u p e)"), ALU.mult, ALU.mult
             )
-            return turn_pairs("w%d" % x, 2 + x, w)
+            words = w[:].bitcast(F32)
+            grouped = tile("w_grp%d" % x, [P, P, PACK], BF16)
+            turn_pairs("w%d" % x, 2 + x, [words[:, u * P : (u + 1) * P] for u in range(2)], grouped[:])
+            return grouped[:]
 
-        v_grp = [gather_values(0)]
-        exps = [exponentials(x) for x in range(QT)]
-        v_grp.append(gather_values(1))
-        w_grp = [weights(x, *exps[x]) for x in range(QT)]
-        v_q = [quantize("v%d" % t, v_grp[t], P) for t in range(2)]
-        v_grp.append(gather_values(2))
-        w_q = [quantize("w%d" % x, w_grp[x], P) for x in range(QT)]
-        v_grp.append(gather_values(3))
-        v_q.append(quantize("v2", v_grp[2], P))
+        def turn_values(t, picked, grouped):
+            words = picked[:].bitcast(F32)
+            turn_pairs("v%d" % t, 6 + t % 2, [words[:, u : I // 2 : 2] for u in range(2)], grouped)
+            return grouped
 
-        o_ps = [bank(x, "o_ps%d" % x, [P, PACK, P]) for x in range(QT)]
-        o_early = tile("o_early", [P, PACK - 1, Q], F32)
-        o_last = tile("o_last", [P, Q], F32)
-        out_rows = out_0.rearrange("(p t) q -> p t q", t=PACK)
+        picked = [gather_values(0), gather_values(1)]
+        neg_max = tile("neg_max", [P, QT], F32, "v_pool1")
+        total = tile("total", [P, QT], F32)
+        p = [exponentials(x, neg_max[:, x : x + 1], total[:, x : x + 1]) for x in range(QT)]
+        v_first = tile("v_first", [P, 2, P, PACK], BF16, "v_pool1")
+        v_grp = [turn_values(t, picked[t], v_first[:, t]) for t in range(2)]
+        v_third = tile("v_third", [P, P, PACK], BF16)
+        v_grp.append(turn_values(2, gather_values(2), v_third[:]))
+        inv = tile("inv", [P, QT], F32, "v_pool2")
+        nc.vector.reciprocal(inv[:], total[:])
+        w_grp = [weights(x, p[x], inv[:, x : x + 1]) for x in range(QT)]
+        v_last = tile("v_last", [P, P, PACK], BF16)
+        v_grp.append(turn_values(3, gather_values(3), v_last[:]))
 
-        def product(x, t):
+        late_codes = tile("late_codes", [P, Q + E], U32, "v_pool3")
+        late_scales = tile("late_scales", [P, Q + E], U8)
+
+        def quantize_late(start, grouped):
+            cols = slice(start, start + P)
+            nc.vector.quantize_mx(
+                out=late_codes[:, cols].bitcast(FP8X4), scales=late_scales[:, cols],
+                in_=grouped.rearrange("p c t -> p (c t)"),
+            )
+
+        def product(out, t, q_cols):
+            v_cols = slice(Q + t * P, Q + (t + 1) * P)
             nc.tensor.matmul_mx(
-                out=o_ps[x][:, t, :], lhsT=v_q[t][0][:].bitcast(FP8X4), lhsT_scale=v_q[t][1][:],
-                rhs=w_q[x][0][:].bitcast(FP8X4), rhs_scale=w_q[x][1][:], start=True, stop=True,
+                out=out, lhsT=late_codes[:, v_cols].bitcast(FP8X4), lhsT_scale=late_scales[:, v_cols],
+                rhs=late_codes[:, q_cols].bitcast(FP8X4), rhs_scale=late_scales[:, q_cols], start=True, stop=True,
             )
 
-        for x in range(QT):
-            for t in range(PACK - 1):
-                product(x, t)
-            nc.scalar.copy(o_early[:, :, x * P : (x + 1) * P], o_ps[x][:, 0 : PACK - 1, :])
-        nc.sync.dma_start(out_rows[:, 0 : PACK - 1, :], o_early[:])
+        out_rows = out_0.rearrange("(p h t) q -> h p t q", h=2, t=2)
+        o_grp = [tile("o_grp%d" % x, [P, P, PACK], BF16) for x in range(QT)]
+        o_ps = [[bank(4 * h + x, "o_ps%d%d" % (h, x), [P, 2, P]) for x in range(QT)] for h in range(2)]
+        o_sb = [tile("o_sb%d" % h, [P, 2, Q], F32) for h in range(2)]
+        o_codes = tile("o_codes", [P, Q], U32)
+        o_scales = tile("o_scales", [P, Q], U8)
+        copy = [nc.vector.tensor_copy, nc.scalar.copy]
 
-        v_q.append(quantize("v3", v_grp[3], P))
+        def products(h):
+            for t in range(2):
+                quantize_late(Q + (2 * h + t) * P, v_grp[2 * h + t])
+                for x in (1, 0):
+                    product(o_ps[h][x][:, t, :], 2 * h + t, slice(x * P, (x + 1) * P))
+
+        def round_pairs(h, x):
+            copy[x](o_grp[x][:, :, 2 * h : 2 * h + 2], o_ps[h][x][:].rearrange("p t q -> p q t"))
+
         for x in range(QT):
-            product(x, PACK - 1)
-        o_grp = tile("o_grp", [P, Q, PACK], BF16)
-        nc.vector.tensor_copy(o_grp[:, 0:P, :], o_ps[0][:].rearrange("p t q -> p q t"))
-        nc.scalar.copy(o_grp[:, P:Q, :], o_ps[1][:].rearrange("p t q -> p q t"))
-        o_codes, o_scales = quantize("o", o_grp, Q)
+            quantize_late(x * P, w_grp[x])
+        products(0)
+        products(1)
         for x in (1, 0):
-            nc.scalar.copy(o_last[:, x * P : (x + 1) * P], o_ps[x][:, PACK - 1, :])
-        nc.scalar.dma_start(out_rows[:, PACK - 1, :], o_last[:])
+            round_pairs(0, x)
+            copy[x](o_sb[0][:, :, x * P : (x + 1) * P], o_ps[0][x][:])
+        nc.sync.dma_start(out_rows[0], o_sb[0][:])
+        for x in (1, 0):
+            round_pairs(1, x)
+            copy[x](o_sb[1][:, :, x * P : (x + 1) * P], o_ps[1][x][:])
+        for x in (1, 0):
+            cols = slice(x * P, (x + 1) * P)
+            nc.vector.quantize_mx(
+                out=o_codes[:, cols].bitcast(FP8X4), scales=o_scales[:, cols],
+                in_=o_grp[x][:].rearrange("p c t -> p (c t)"),
+            )
+        nc.scalar.dma_start(out_rows[1], o_sb[1][:])
         nc.sync.dma_start(out_1[0].rearrange("p c r -> p (c r)").bitcast(I32), o_codes[:].bitcast(I32))
         for quad in range(4):
             queue = nc.sync if quad < 2 else nc.scalar

@@ -188,7 +188,11 @@ def tile_attend_bestofviews_pl_kernel(
             turn_pairs("v%d" % t, 6 + t % 2, [words[:, u : I // 2 : 2] for u in range(2)], grouped)
             return grouped
 
-        picked = [gather_values(0), gather_values(1)]
+        v0_pool = tile("v0_pool", [P, T], BF16)
+        nc.gpsimd.tensor_copy(v0_pool[:], v_pool[0][:])
+        picked0 = tile("v_picked0", [P, I], BF16, "half_a3")
+        nc.scalar.activation(picked0[:], v0_pool[:].indirect(offsets[:]), ACT.Copy)
+        picked = [picked0, gather_values(1)]
         neg_max = tile("neg_max", [P, QT], F32, "v_pool1")
         total = tile("total", [P, QT], F32)
         p = [exponentials(x, neg_max[:, x : x + 1], total[:, x : x + 1]) for x in range(QT)]

from contextlib import ExitStack

import concourse.mybir as mybir
from concourse.masks import make_identity

D, T, I, Q, E, K = 512, 2048, 512, 256, 512, 512
FLOPS = 2 * Q * I * (D + K + E)

F32 = mybir.dt.float32
BF16 = mybir.dt.bfloat16
I32 = mybir.dt.int32
U32 = mybir.dt.uint32
U16 = mybir.dt.uint16
U8 = mybir.dt.uint8
FP8X4 = mybir.dt.float8_e4m3fn_x4
FP4X4 = mybir.dt.float4_e2m1fn_x4
ALU = mybir.AluOpType
ACT = mybir.ActivationFunctionType
AXIS_X = mybir.AxisListType.X

P = 128
PACK = 4
QT = Q // P
ST = I // P
HALF = I // 2


def tile_attend_bestofviews_pl_kernel(
    tc, query, query2, keys_words, keys_scales, keys2, size, vals, offs, out_0, out_1, out_2
):
    nc = tc.nc
    with ExitStack() as ctx:
        sb = ctx.enter_context(tc.tile_pool(name="sb", bufs=1))
        ps = ctx.enter_context(tc.psum_pool(name="ps", bufs=1))

        def tile(name, shape, dtype, after=None):
            return sb.tile(shape, dtype, name=name, tag=after or name, align_bytes=64)

        def bank(n, name, shape):
            return ps.tile(shape, F32, name=name, tag="bank%d" % n)

        def quantize(name, grouped, width, after=None):
            codes = tile(name + "_codes", [P, width], U32, after)
            scales = tile(name + "_scales", [P, width], U8)
            nc.vector.quantize_mx(
                out=codes[:].bitcast(FP8X4), scales=scales[:], in_=grouped[:].rearrange("p c t -> p (c t)")
            )
            return codes, scales

        def interleave(dst, src):
            nc.scalar.copy(
                dst.rearrange("p (c i) t -> p c t i", i=4), src.rearrange("p t (c i) -> p c t i", i=4)
            )

        offsets = sb.tile([P, I // 16], U16, name="offsets")
        kw_pool = tile("kw_pool", [P, T], U16)
        ks_pool = tile("ks_pool", [P, T], U8)
        size_col = tile("size_col", [P, PACK], F32)
        q_raw = tile("q_raw", [P, PACK, Q], F32)
        q2_raw = tile("q2_raw", [P, PACK, Q], F32)
        k2_pool = [tile("k2_pool%d" % t, [P, T], F32) for t in range(PACK)]
        v_pool = [tile("v_pool%d" % t, [P, T], F32) for t in range(PACK)]
        k2_rows = keys2.rearrange("(p t) c -> t p c", t=PACK)
        v_rows = vals.rearrange("(p t) c -> t p c", t=PACK)

        nc.sync.dma_start(kw_pool[:].bitcast(I32), keys_words[0].bitcast(I32))
        nc.sync.dma_start(offsets[:], offs)
        nc.sync.dma_start(q_raw[:], query.rearrange("(p t) q -> p t q", t=PACK))
        nc.sync.dma_start(size_col[:], size[0].rearrange("(p t) -> p t", t=PACK))
        for t in range(PACK):
            nc.sync.dma_start(k2_pool[t][:], k2_rows[t])
        nc.sync.dma_start(q2_raw[:], query2.rearrange("(p t) q -> p t q", t=PACK))
        for t in range(PACK):
            nc.sync.dma_start(v_pool[t][:], v_rows[t])

        nc.vector.memset(ks_pool[:].bitcast(I32), 0)
        for quad in range(4):
            nc.scalar.dma_start(
                ks_pool[32 * quad : 32 * quad + 4, :].bitcast(I32),
                keys_scales[0, 4 * quad : 4 * quad + 4, :].bitcast(I32),
            )
        ident = tile("ident", [P, P], F32)
        make_identity(nc, ident[:])

        kw = tile("kw", [P, I], U16)
        nc.vector.tensor_copy(kw[:], kw_pool[:].indirect(offsets[:]))
        q_grp = tile("q_grp", [P, Q, PACK], BF16)
        interleave(q_grp[:], q_raw[:])
        q_codes, q_scales = quantize("q", q_grp, Q)
        ks = tile("ks", [P, I], U8)
        nc.vector.tensor_copy(ks[:], ks_pool[:].indirect(offsets[:]))

        size_ps = bank(6, "size_ps", [P, PACK, P])
        for t in range(PACK):
            nc.tensor.transpose(size_ps[:, t, :], size_col[:, t : t + 1].to_broadcast([P, P]), ident[:])
        size_row = tile("size_row", [P, 2, P, 2], F32)
        nc.scalar.copy(size_row[:], size_ps[:].rearrange("m (u e) p -> m u p e", u=2))

        s_ps = [bank(4 + x, "s_ps%d" % x, [P, I]) for x in range(QT)]
        half_a = [tile("half_a%d" % j, [P, Q], F32) for j in range(ST)]
        for j in range(ST):
            cols = slice(j * P, (j + 1) * P)
            a_ps = bank(j, "a_ps%d" % j, [P, Q])
            nc.tensor.matmul_mx(
                out=a_ps[:], lhsT=kw[:, cols].bitcast(FP4X4), lhsT_scale=ks[:, cols],
                rhs=q_codes[:].bitcast(FP8X4), rhs_scale=q_scales[:], start=True, stop=True,
            )
            nc.scalar.activation(half_a[j][:], a_ps[:], ACT.Copy, scale=0.5)

        def add_turned(x, j, src, start, stop):
            nc.tensor.matmul(
                s_ps[x][:, j * P : (j + 1) * P], src[:, x * P : (x + 1) * P], ident[:],
                start=start, stop=stop, is_transpose=True,
            )

        for x in range(QT):
            for j in range(ST):
                add_turned(x, j, half_a[j], j == 0, False)

        k2_grp = [tile("k2_grp%d" % h, [P, HALF, PACK], BF16) for h in range(2)]
        for t in range(PACK):
            for h in range(2):
                nc.vector.tensor_copy(
                    k2_grp[h][:, :, t], k2_pool[t][:].indirect(offsets[:, h * 16 : (h + 1) * 16])
                )
        k2_q = [quantize("k2_%d" % h, k2_grp[h], HALF) for h in range(2)]
        q2_codes = tile("q2_codes", [P, Q], U32)
        q2_scales = tile("q2_scales", [P, Q], U8)
        for x in range(QT):
            cols = slice(x * P, (x + 1) * P)
            q2_grp = tile("q2_grp%d" % x, [P, P, PACK], BF16)
            interleave(q2_grp[:], q2_raw[:, :, cols])
            nc.vector.quantize_mx(
                out=q2_codes[:, cols].bitcast(FP8X4), scales=q2_scales[:, cols],
                in_=q2_grp[:].rearrange("p c t -> p (c t)"),
            )

        half_b = [tile("half_b%d" % j, [P, Q], F32) for j in range(ST)]
        half_m = [tile("half_m%d" % j, [P, Q], F32) for j in range(ST)]
        for j in range(ST):
            codes, scales = k2_q[j // 2]
            cols = slice((j % 2) * P, (j % 2 + 1) * P)
            b_ps = bank(j, "b_ps%d" % j, [P, Q])
            nc.tensor.matmul_mx(
                out=b_ps[:], lhsT=codes[:, cols].bitcast(FP8X4), lhsT_scale=scales[:, cols],
                rhs=q2_codes[:].bitcast(FP8X4), rhs_scale=q2_scales[:], start=True, stop=True,
            )
            nc.vector.scalar_tensor_tensor(half_m[j][:], b_ps[:], 0.5, half_a[j][:], ALU.mult, ALU.max)
            nc.scalar.activation(half_b[j][:], b_ps[:], ACT.Copy, scale=0.5)
        for x in range(QT):
            for j in range(ST):
                add_turned(x, j, half_m[j], False, False)
                add_turned(x, j, half_b[j], False, j == ST - 1)

        def turn_pairs(name, n, halves, grouped):
            turned = bank(n, name + "_ps", [P, 2, P])
            for u in range(2):
                nc.tensor.transpose(turned[:, u, :], halves[u], ident[:])
            nc.scalar.copy(grouped.bitcast(F32), turned[:].rearrange("p u c -> p c u"))

        def gather_values(t, after=None):
            picked = tile("v_picked%d" % t, [P, I], BF16)
            nc.vector.tensor_copy(picked[:], v_pool[t][:].indirect(offsets[:]))
            return picked

        def exponentials(x, neg_max, total):
            nc.vector.tensor_reduce(neg_max, s_ps[x][:], AXIS_X, ALU.max, negate=True)
            p = tile("p%d" % x, [P, I], F32)
            nc.scalar.activation(
                p[:].rearrange("m (u p e) -> m u p e", u=2, e=2),
                s_ps[x][:].rearrange("m (p u e) -> m u p e", u=2, e=2),
                ACT.Exp, bias=neg_max, accum_out=total,
            )
            return p

        def weights(x, p, inv):
            w = tile("w%d" % x, [P, I], BF16)
            nc.vector.scalar_tensor_tensor(
                w[:], p[:], inv, size_row[:].rearrange("m u p e -> m (u p e)"), ALU.mult, ALU.mult
            )
            words = w[:].bitcast(F32)
            grouped = tile("w_grp%d" % x, [P, P, PACK], BF16)
            turn_pairs("w%d" % x, 2 + x, [words[:, u * P : (u + 1) * P] for u in range(2)], grouped[:])
            return grouped[:]

        def turn_values(t, picked, grouped):
            words = picked[:].bitcast(F32)
            turn_pairs("v%d" % t, 6 + t % 2, [words[:, u : I // 2 : 2] for u in range(2)], grouped)
            return grouped

        v0_pool = tile("v0_pool", [P, T], BF16)
        nc.gpsimd.tensor_copy(v0_pool[:], v_pool[0][:])
        picked0 = tile("v_picked0", [P, I], BF16, "half_a3")
        nc.scalar.activation(picked0[:], v0_pool[:].indirect(offsets[:]), ACT.Copy)
        picked = [picked0, gather_values(1)]
        neg_max = tile("neg_max", [P, QT], F32, "v_pool1")
        total = tile("total", [P, QT], F32)
        p = [exponentials(x, neg_max[:, x : x + 1], total[:, x : x + 1]) for x in range(QT)]
        v_first = tile("v_first", [P, 2, P, PACK], BF16, "v_pool1")
        v_grp = [turn_values(t, picked[t], v_first[:, t]) for t in range(2)]
        v_third = tile("v_third", [P, P, PACK], BF16)
        v_grp.append(turn_values(2, gather_values(2), v_third[:]))
        inv = tile("inv", [P, QT], F32, "v_pool2")
        nc.vector.reciprocal(inv[:], total[:])
        w_grp = [weights(x, p[x], inv[:, x : x + 1]) for x in range(QT)]
        v_last = tile("v_last", [P, P, PACK], BF16)
        v_grp.append(turn_values(3, gather_values(3), v_last[:]))

        late_codes = tile("late_codes", [P, Q + E], U32, "v_pool3")
        late_scales = tile("late_scales", [P, Q + E], U8)

        def quantize_late(start, grouped):
            cols = slice(start, start + P)
            nc.vector.quantize_mx(
                out=late_codes[:, cols].bitcast(FP8X4), scales=late_scales[:, cols],
                in_=grouped.rearrange("p c t -> p (c t)"),
            )

        def product(out, t, q_cols):
            v_cols = slice(Q + t * P, Q + (t + 1) * P)
            nc.tensor.matmul_mx(
                out=out, lhsT=late_codes[:, v_cols].bitcast(FP8X4), lhsT_scale=late_scales[:, v_cols],
                rhs=late_codes[:, q_cols].bitcast(FP8X4), rhs_scale=late_scales[:, q_cols], start=True, stop=True,
            )

        out_rows = out_0.rearrange("(p h t) q -> h p t q", h=2, t=2)
        o_grp = [tile("o_grp%d" % x, [P, P, PACK], BF16) for x in range(QT)]
        o_ps = [[bank(4 * h + x, "o_ps%d%d" % (h, x), [P, 2, P]) for x in range(QT)] for h in range(2)]
        o_sb = [tile("o_sb%d" % h, [P, 2, Q], F32) for h in range(2)]
        o_codes = tile("o_codes", [P, Q], U32)
        o_scales = tile("o_scales", [P, Q], U8)
        copy = [nc.vector.tensor_copy, nc.scalar.copy]

        def products(h):
            for t in range(2):
                quantize_late(Q + (2 * h + t) * P, v_grp[2 * h + t])
                for x in (1, 0):
                    product(o_ps[h][x][:, t, :], 2 * h + t, slice(x * P, (x + 1) * P))

        def round_pairs(h, x):
            copy[x](o_grp[x][:, :, 2 * h : 2 * h + 2], o_ps[h][x][:].rearrange("p t q -> p q t"))

        for x in range(QT):
            quantize_late(x * P, w_grp[x])
        products(0)
        products(1)
        for x in (1, 0):
            round_pairs(0, x)
            copy[x](o_sb[0][:, :, x * P : (x + 1) * P], o_ps[0][x][:])
        nc.sync.dma_start(out_rows[0], o_sb[0][:])
        for x in (1, 0):
            round_pairs(1, x)
            copy[x](o_sb[1][:, :, x * P : (x + 1) * P], o_ps[1][x][:])
        for x in (1, 0):
            cols = slice(x * P, (x + 1) * P)
            nc.vector.quantize_mx(
                out=o_codes[:, cols].bitcast(FP8X4), scales=o_scales[:, cols],
                in_=o_grp[x][:].rearrange("p c t -> p (c t)"),
            )
        nc.scalar.dma_start(out_rows[1], o_sb[1][:])
        nc.sync.dma_start(out_1[0].rearrange("p c r -> p (c r)").bitcast(I32), o_codes[:].bitcast(I32))
        for quad in range(4):
            queue = nc.sync if quad < 2 else nc.scalar
            queue.dma_start(
                out_2[0, 4 * quad : 4 * quad + 4, :].bitcast(I32),
                o_scales[32 * quad : 32 * quad + 4, :].bitcast(I32),
            )
